import numpy as np
import ml_dtypes


def mxq(x, axis, fmt="e4m3"):
    dtype, down = {"e4m3": (ml_dtypes.float8_e4m3fn, 7), "e5m2": (ml_dtypes.float8_e5m2, 14)}[fmt]
    v = np.moveaxis(np.asarray(x, np.float32).astype(ml_dtypes.bfloat16).astype(np.float64), axis, -1)
    blocks = v.reshape(v.shape[:-1] + (-1, 32))
    amax = np.abs(blocks).max(-1, keepdims=True)
    byte = np.maximum(np.where(amax > 0, np.frexp(amax)[1] - 1 + 127, 0) - down, 1)
    scale = np.exp2(byte - 127.0)
    codes = (blocks / scale).astype(np.float32).astype(dtype).astype(np.float64)
    return np.moveaxis((codes * scale).reshape(v.shape), -1, axis)


WIDE = False


def mx_kscale(k):
    if not WIDE:
        return np.ones(k)
    levels = np.array([30, -30])
    if k % 512:
        return np.exp2(np.random.permutation(np.resize(levels, k // 32))).repeat(32)
    a = np.empty((k // 512, 16))
    for p in range(k // 512):
        a[p, :8] = np.random.permutation(np.resize(levels, 8))
        for g in range(8):
            far = levels[np.abs(levels - a[p, g]) >= 10]
            a[p, g + 8] = far[np.random.randint(len(far))]
    return np.exp2(a.ravel()).repeat(32)


def f64(x):
    return np.asarray(x).astype(np.float64)


def striped(idx):
    return np.tile(np.asarray(idx).reshape(-1, 16).T, (8, 1)).astype(np.uint16)


def unstriped(offs):
    return offs[:16].T.reshape(-1).astype(np.int64)


E2M1 = np.array([0.0, 0.5, 1.0, 1.5, 2.0, 3.0, 4.0, 6.0, -0.0, -0.5, -1.0, -1.5, -2.0, -3.0, -4.0, -6.0])


def pack_weight(w, fmt):
    k, n = w.shape
    w = f64(np.asarray(w, np.float32).astype(ml_dtypes.bfloat16)).reshape(k // 32, 32, n)
    amax = np.abs(w).max(1)
    if fmt == "e4m3":
        byte = np.frexp(amax)[1] - 1 + 127 - 7
    else:
        mant, ex = np.frexp(amax / 6.0)
        byte = np.where(mant > 0.5, ex, ex - 1) + 127
    byte = np.clip(np.where(amax > 0, byte, 1), 1, 254)
    scaled = (w * np.exp2(127.0 - byte)[:, None, :]).reshape(k, n).astype(np.float32)
    by_word = np.ascontiguousarray(scaled.reshape(k // 512, 128, 4, n).transpose(0, 1, 3, 2))
    if fmt == "e4m3":
        words = by_word.astype(ml_dtypes.float8_e4m3fn).view(np.uint8)
    else:
        c = by_word.astype(ml_dtypes.float4_e2m1fn).view(np.uint8) & 0xF
        words = (c[..., 0::2] | (c[..., 1::2] << 4)).reshape(k // 512, 128, 2 * n)
    return np.ascontiguousarray(words), np.ascontiguousarray(byte.astype(np.uint8).reshape(k // 512, 16, n))


def unpack_weight(words, scales, fmt):
    g, _, n = scales.shape
    words = np.ascontiguousarray(words).reshape(g, 128, n, -1)
    if fmt == "e4m3":
        vals = words.view(ml_dtypes.float8_e4m3fn).astype(np.float64)
    else:
        nib = np.empty((g, 128, n, 4), np.uint8)
        nib[..., 0::2] = words & 0xF
        nib[..., 1::2] = words >> 4
        vals = E2M1[nib]
    vals = vals * np.repeat(np.exp2(scales.astype(np.float64) - 127.0), 8, axis=1)[..., None]
    return vals.transpose(0, 1, 3, 2).reshape(g * 512, n)


K, R, N, T, J, V = 512, 512, 512, 1024, 512, 1024


def setup_inputs():
    n = np.random.standard_normal
    idx = np.random.permutation(T)[:J]
    idx2 = np.random.permutation(V)[:J]
    fn = mx_kscale(N)
    fr = mx_kscale(R)
    wdp = pack_weight(n((N, R)) * 1 / np.sqrt(N) * fn[:, None] * fr, "e2m1")
    wup = pack_weight(n((R, K)) * 1 / np.sqrt(R) / fr[:, None], "e4m3")
    return {
        "g": (n((N, T)) * np.exp(0.5 * n((1, T))) / fn[:, None]).astype(np.float32),
        "wd_words": wdp[0],
        "wd_scales": wdp[1],
        "tb": (n((R, V)) * 0.5 * fr[:, None]).astype(np.float32),
        "wu_words": wup[0],
        "wu_scales": wup[1],
        "offs": striped(idx),
        "offs2": striped(idx2),
    }


def reference(g, wd_words, wd_scales, tb, wu_words, wu_scales, offs, offs2):
    idx = unstriped(offs)
    idx2 = unstriped(offs2)
    wdu = unpack_weight(wd_words, wd_scales, "e2m1")
    wuu = unpack_weight(wu_words, wu_scales, "e4m3")
    gidxq = mxq(f64(g)[:, idx], 0, "e5m2")
    dh = wdu.T @ gidxq
    dz = dh - f64(tb)[:, idx2]
    dzq = mxq(dz, 0, "e5m2")
    y = wuu.T @ dzq
    return y

@@ -1,0 +1,153 @@
+from contextlib import ExitStack
+
+import concourse.mybir as mybir
+
+K, R, N, T, J, V = 512, 512, 512, 1024, 512, 1024
+FLOPS = 2 * N * R * J + 2 * R * K * J
+
+F32 = mybir.dt.float32
+BF16 = mybir.dt.bfloat16
+I32 = mybir.dt.int32
+U32 = mybir.dt.uint32
+U16 = mybir.dt.uint16
+U8 = mybir.dt.uint8
+E5M2 = mybir.dt.float8_e5m2_x4
+E4M3 = mybir.dt.float8_e4m3fn_x4
+E2M1 = mybir.dt.float4_e2m1fn_x4
+COPY = mybir.ActivationFunctionType.Copy
+SUB = mybir.AluOpType.subtract
+MULT = mybir.AluOpType.mult
+
+P = 128
+PACK = 4
+RUN = 4
+HALF = J // 2
+
+
+def woven(dst, src, c0, c1):
+    d = dst[:, c0:c1, :].rearrange("p (c i) t -> p c t i", i=RUN)
+    s = src[:, :, c0:c1].rearrange("p t (c i) -> p c t i", i=RUN)
+    return d, s
+
+
+def tile_list_gradient_less_table_kernel(tc, g, wd_words, wd_scales, tb, wu_words, wu_scales, offs, offs2, out):
+    nc = tc.nc
+    with ExitStack() as ctx:
+        keep = ctx.enter_context(tc.tile_pool(name="keep", bufs=1))
+        psum = ctx.enter_context(tc.psum_pool(name="psum", bufs=1))
+
+        idx = keep.tile([P, J // 16], U16, name="idx")
+        idx2 = keep.tile([P, J // 16], U16, name="idx2")
+        wd_raw = keep.tile([P, 2 * R], U8, name="wd_raw", align_bytes=64)
+        wd_sraw = keep.tile([P, R], U8, name="wd_sraw", align_bytes=64)
+        wd_c = keep.tile([P, 2 * R], U8, name="wd_c", align_bytes=64)
+        wd_s = keep.tile([P, R], U8, name="wd_s", align_bytes=64)
+        wu_c = keep.tile([P, K], U32, name="wu_c", align_bytes=64)
+        wu_s = keep.tile([P, K], U8, name="wu_s", align_bytes=64)
+        g_pl = [keep.tile([P, T], F32, name=f"g{t}") for t in range(PACK)]
+        tb_pl = [keep.tile([P, V], F32, name=f"tb{t}") for t in range(PACK)]
+
+        g_rows = g.rearrange("(p t) c -> t p c", t=PACK)
+        tb_rows = tb.rearrange("(p t) c -> t p c", t=PACK)
+
+        nc.vector.memset(wd_sraw[:].bitcast(I32), 0)
+        nc.gpsimd.memset(wu_s[:].bitcast(I32), 0)
+        nc.sync.dma_start(idx[:], offs)
+        nc.sync.dma_start(wd_raw[:].bitcast(I32), wd_words[0].bitcast(I32))
+        for q in range(4):
+            nc.scalar.dma_start(wd_sraw[32 * q : 32 * q + 4, :].bitcast(I32), wd_scales[0, 4 * q : 4 * q + 4, :].bitcast(I32))
+        for t in range(PACK):
+            nc.sync.dma_start(g_pl[t][:], g_rows[t])
+        nc.sync.dma_start(idx2[:], offs2)
+        for t in range(PACK):
+            nc.sync.dma_start(tb_pl[t][:], tb_rows[t])
+        nc.sync.dma_start(wu_c[:].bitcast(I32), wu_words[0].rearrange("p n t -> p (n t)").bitcast(I32))
+        for q in range(4):
+            nc.sync.dma_start(wu_s[32 * q : 32 * q + 4, :].bitcast(I32), wu_scales[0, 4 * q : 4 * q + 4, :].bitcast(I32))
+
+        nc.vector.tensor_copy(
+            wd_c[:].bitcast(U16).rearrange("p (t m) -> p t m", t=PACK),
+            wd_raw[:].bitcast(U16).rearrange("p (m t) -> p t m", t=PACK),
+        )
+        nc.vector.tensor_copy(
+            wd_s[:].rearrange("p (t m) -> p t m", t=PACK),
+            wd_sraw[:].rearrange("p (m t) -> p t m", t=PACK),
+        )
+
+        g_pick = keep.tile([P, PACK, J], BF16, name="g_pick", align_bytes=64)
+        g_wov = keep.tile([P, J, PACK], BF16, name="g_wov", tag="shared", align_bytes=64)
+        for t in range(PACK):
+            nc.vector.tensor_copy(g_pick[:, t, :], g_pl[t][:].indirect(idx[:]))
+        split = 352
+        d, s = woven(g_wov, g_pick, 0, split)
+        nc.vector.tensor_copy(d, s)
+        d, s = woven(g_wov, g_pick, split, J)
+        nc.scalar.copy(d, s)
+        gq_c = keep.tile([P, J], U32, name="gq_c", align_bytes=64)
+        gq_s = keep.tile([P, J], U8, name="gq_s", align_bytes=64)
+        nc.vector.quantize_mx(gq_c[:].bitcast(E5M2), gq_s[:], g_wov[:].rearrange("p j t -> p (j t)"))
+
+        dh = [psum.tile([P, J], F32, name=f"dh{t}") for t in range(PACK)]
+        for t in (1, 2, 3, 0):
+            nc.tensor.matmul_mx(
+                dh[t][:],
+                lhsT=wd_c[:, 2 * P * t : 2 * P * (t + 1)].bitcast(E2M1),
+                lhsT_scale=wd_s[:, P * t : P * (t + 1)],
+                rhs=gq_c[:].bitcast(E5M2),
+                rhs_scale=gq_s[:],
+                start=True,
+                stop=True,
+            )
+
+        halves = [slice(0, HALF), slice(HALF, J)]
+        lists = [idx2[:, 0 : HALF // 16], idx2[:, HALF // 16 : J // 16]]
+        tb0 = keep.tile([P, J], F32, name="tb0_pick", tag="shared", align_bytes=64)
+        nc.vector.tensor_copy(tb0[:], tb_pl[0][:].indirect(idx2[:]))
+        dh_sb = [keep.tile([P, J], F32, name=f"dh_sb{t}") for t in range(1, PACK)]
+        for t in range(1, PACK):
+            for h in range(2):
+                nc.scalar.copy(dh_sb[t - 1][:, halves[h]], dh[t][:, halves[h]])
+
+        ndz = [keep.tile([P, PACK, HALF], F32, name=f"ndz{h}", align_bytes=64) for h in range(2)]
+        dz_wov = [keep.tile([P, HALF, PACK], BF16, name=f"dz_wov{h}", align_bytes=64) for h in range(2)]
+        dq_c = keep.tile([P, J], U32, name="dq_c", align_bytes=64)
+        dq_s = keep.tile([P, J], U8, name="dq_s", align_bytes=64)
+
+        def differences(h):
+            for t in range(1, PACK):
+                nc.vector.tensor_tensor(ndz[h][:, t, :], tb_pl[t][:].indirect(lists[h]), dh_sb[t - 1][:, halves[h]], SUB)
+            nc.vector.tensor_tensor(ndz[h][:, 0, :], tb0[:, halves[h]], dh[0][:, halves[h]], SUB)
+
+        def quantise(h):
+            nc.vector.quantize_mx(dq_c[:, halves[h]].bitcast(E5M2), dq_s[:, halves[h]], dz_wov[h][:].rearrange("p j t -> p (j t)"))
+
+        differences(0)
+        d, s = woven(dz_wov[0], ndz[0], 0, HALF)
+        nc.scalar.activation(d, s, COPY, scale=-1.0)
+        differences(1)
+        split = 176
+        d, s = woven(dz_wov[1], ndz[1], 0, split)
+        nc.vector.tensor_scalar(d, s, -1.0, None, MULT)
+        d, s = woven(dz_wov[1], ndz[1], split, HALF)
+        nc.scalar.activation(d, s, COPY, scale=-1.0)
+        quantise(0)
+        quantise(1)
+
+        y = [psum.tile([P, J], F32, name=f"y{c}") for c in range(K // P)]
+        y_sb = [keep.tile([P, J], F32, name=f"y_sb{c}") for c in range(K // P)]
+        for c in range(K // P):
+            cols = slice(P * c, P * (c + 1))
+            nc.tensor.matmul_mx(
+                y[c][:],
+                lhsT=wu_c[:, cols].bitcast(E4M3),
+                lhsT_scale=wu_s[:, cols],
+                rhs=dq_c[:].bitcast(E5M2),
+                rhs_scale=dq_s[:],
+                start=True,
+                stop=True,
+            )
+            if c % 2 == 0:
+                nc.scalar.copy(y_sb[c][:], y[c][:])
+            else:
+                nc.vector.tensor_copy(y_sb[c][:], y[c][:])
+            nc.sync.dma_start(out[cols, :], y_sb[c][:])

@@ -22,11 +22,13 @@ P = 128
 PACK = 4
 RUN = 4
 HALF = J // 2
+QUARTER = J // 4
+LAST = PACK - 1
 
 
-def woven(dst, src, c0, c1):
-    d = dst[:, c0:c1, :].rearrange("p (c i) t -> p c t i", i=RUN)
-    s = src[:, :, c0:c1].rearrange("p t (c i) -> p c t i", i=RUN)
+def woven(dst, src):
+    d = dst.rearrange("p (c i) t -> p c t i", i=RUN)
+    s = src.rearrange("p t (c i) -> p c t i", i=RUN)
     return d, s
 
 
@@ -40,114 +42,144 @@ def tile_list_gradient_less_table_kernel(tc, g, wd_words, wd_scales, tb, wu_word
         idx2 = keep.tile([P, J // 16], U16, name="idx2")
         wd_raw = keep.tile([P, 2 * R], U8, name="wd_raw", align_bytes=64)
         wd_sraw = keep.tile([P, R], U8, name="wd_sraw", align_bytes=64)
-        wd_c = keep.tile([P, 2 * R], U8, name="wd_c", align_bytes=64)
-        wd_s = keep.tile([P, R], U8, name="wd_s", align_bytes=64)
         wu_c = keep.tile([P, K], U32, name="wu_c", align_bytes=64)
         wu_s = keep.tile([P, K], U8, name="wu_s", align_bytes=64)
-        g_pl = [keep.tile([P, T], F32, name=f"g{t}") for t in range(PACK)]
+        g_pl = [keep.tile([P, T], F32, name=f"g{t}", tag=f"g{t}", align_bytes=64) for t in range(PACK)]
         tb_pl = [keep.tile([P, V], F32, name=f"tb{t}") for t in range(PACK)]
+        dq_c = keep.tile([P, HALF + J], U32, name="dq_c", align_bytes=64)
+        dq_s = keep.tile([P, HALF + J], U8, name="dq_s", align_bytes=64)
 
         g_rows = g.rearrange("(p t) c -> t p c", t=PACK)
         tb_rows = tb.rearrange("(p t) c -> t p c", t=PACK)
+        halves = [slice(0, HALF), slice(HALF, J)]
+        list_halves = [slice(0, HALF // 16), slice(HALF // 16, J // 16)]
 
         nc.vector.memset(wd_sraw[:].bitcast(I32), 0)
         nc.gpsimd.memset(wu_s[:].bitcast(I32), 0)
-        nc.sync.dma_start(idx[:], offs)
-        nc.sync.dma_start(wd_raw[:].bitcast(I32), wd_words[0].bitcast(I32))
+        nc.gpsimd.memset(dq_c[:, 0:HALF], 0)
+        nc.gpsimd.memset(dq_s[:, 0:HALF].bitcast(I32), 0)
         for q in range(4):
             nc.scalar.dma_start(wd_sraw[32 * q : 32 * q + 4, :].bitcast(I32), wd_scales[0, 4 * q : 4 * q + 4, :].bitcast(I32))
         for t in range(PACK):
             nc.sync.dma_start(g_pl[t][:], g_rows[t])
+            if t == 0:
+                nc.sync.dma_start(idx[:], offs)
+        nc.sync.dma_start(wd_raw[:].bitcast(I32), wd_words[0].bitcast(I32))
         nc.sync.dma_start(idx2[:], offs2)
-        for t in range(PACK):
+        for t in (LAST, 0, 1, 2):
             nc.sync.dma_start(tb_pl[t][:], tb_rows[t])
         nc.sync.dma_start(wu_c[:].bitcast(I32), wu_words[0].rearrange("p n t -> p (n t)").bitcast(I32))
         for q in range(4):
             nc.sync.dma_start(wu_s[32 * q : 32 * q + 4, :].bitcast(I32), wu_scales[0, 4 * q : 4 * q + 4, :].bitcast(I32))
 
-        nc.vector.tensor_copy(
-            wd_c[:].bitcast(U16).rearrange("p (t m) -> p t m", t=PACK),
-            wd_raw[:].bitcast(U16).rearrange("p (m t) -> p t m", t=PACK),
-        )
-        nc.vector.tensor_copy(
-            wd_s[:].rearrange("p (t m) -> p t m", t=PACK),
-            wd_sraw[:].rearrange("p (m t) -> p t m", t=PACK),
-        )
+        wd_by_t = wd_raw[:].bitcast(U16).rearrange("p (m t) -> p t m", t=PACK)
+        wd_s_by_t = wd_sraw[:].rearrange("p (m t) -> p t m", t=PACK)
 
-        g_pick = keep.tile([P, PACK, J], BF16, name="g_pick", align_bytes=64)
-        g_wov = keep.tile([P, J, PACK], BF16, name="g_wov", tag="shared", align_bytes=64)
-        for t in range(PACK):
-            nc.vector.tensor_copy(g_pick[:, t, :], g_pl[t][:].indirect(idx[:]))
-        split = 352
-        d, s = woven(g_wov, g_pick, 0, split)
-        nc.vector.tensor_copy(d, s)
-        d, s = woven(g_wov, g_pick, split, J)
-        nc.scalar.copy(d, s)
+        g_pick = keep.tile([P, PACK, J], BF16, name="g_pick", tag="g_pick", align_bytes=64)
+        g_wov_tile = keep.tile([P, J * PACK], BF16, name="g_wov", tag="g_wov", align_bytes=64)
+        g_wov = [g_wov_tile[:, h * HALF * PACK : (h + 1) * HALF * PACK].rearrange("p (j t) -> p j t", t=PACK) for h in range(2)]
         gq_c = keep.tile([P, J], U32, name="gq_c", align_bytes=64)
         gq_s = keep.tile([P, J], U8, name="gq_s", align_bytes=64)
-        nc.vector.quantize_mx(gq_c[:].bitcast(E5M2), gq_s[:], g_wov[:].rearrange("p j t -> p (j t)"))
+        for t in range(LAST):
+            nc.vector.tensor_copy(g_pick[:, t, :], g_pl[t][:].indirect(idx[:]))
+        for h in range(2):
+            nc.vector.tensor_copy(g_pick[:, LAST, halves[h]], g_pl[LAST][:].indirect(idx[:, list_halves[h]]))
+        wd_c0 = keep.tile([P, 2 * P], U8, name="wd_c0", align_bytes=64)
+        wd_s0 = keep.tile([P, P], U8, name="wd_s0", tag="g3", align_bytes=64)
+        nc.vector.tensor_copy(wd_c0[:].bitcast(U16), wd_by_t[:, 0, :])
+        nc.vector.tensor_copy(wd_s0[:], wd_s_by_t[:, 0, :])
+        nc.scalar.copy(*woven(g_wov[0], g_pick[:, :, halves[0]]))
+        nc.vector.tensor_copy(*woven(g_wov[1], g_pick[:, :, halves[1]]))
+        for h in range(2):
+            nc.vector.quantize_mx(gq_c[:, halves[h]].bitcast(E5M2), gq_s[:, halves[h]], g_wov_tile[:, h * HALF * PACK : (h + 1) * HALF * PACK])
+        wd_rest = keep.tile([P, LAST * 3 * P], U8, name="wd_rest", tag="g_pick", align_bytes=64)
+        wd_c = wd_rest[:, : LAST * 2 * P]
+        wd_s = wd_rest[:, LAST * 2 * P :]
+        nc.vector.tensor_copy(wd_c.bitcast(U16).rearrange("p (t m) -> p t m", t=LAST), wd_by_t[:, 1:, :])
+        nc.vector.tensor_copy(wd_s.rearrange("p (t m) -> p t m", t=LAST), wd_s_by_t[:, 1:, :])
 
         dh = [psum.tile([P, J], F32, name=f"dh{t}") for t in range(PACK)]
-        for t in (1, 2, 3, 0):
+        for t in (0, LAST, 1, 2):
+            codes = wd_c0[:] if t == 0 else wd_c[:, 2 * P * (t - 1) : 2 * P * t]
+            scales = wd_s0[:] if t == 0 else wd_s[:, P * (t - 1) : P * t]
             nc.tensor.matmul_mx(
-                dh[t][:],
-                lhsT=wd_c[:, 2 * P * t : 2 * P * (t + 1)].bitcast(E2M1),
-                lhsT_scale=wd_s[:, P * t : P * (t + 1)],
-                rhs=gq_c[:].bitcast(E5M2),
-                rhs_scale=gq_s[:],
+                dh[t][:], lhsT=codes.bitcast(E2M1), lhsT_scale=scales, rhs=gq_c[:].bitcast(E5M2), rhs_scale=gq_s[:], start=True, stop=True
+            )
+
+        tb_last = keep.tile([P, J], F32, name="tb_last", tag="g_wov", align_bytes=64)
+        nc.vector.tensor_copy(tb_last[:], tb_pl[LAST][:].indirect(idx2[:]))
+
+        slots = keep.tile([P, 7 * HALF + QUARTER], F32, name="slots", align_bytes=64)
+        ndz = [slots[:, first : first + PACK * HALF].rearrange("p (t j) -> p t j", t=PACK) for first in (0, LAST * HALF + QUARTER)]
+        dz_wov = [keep.tile([P, HALF, PACK], BF16, name=f"dz_wov{h}", align_bytes=64) for h in range(2)]
+
+        dh_sb = {(t, h): keep.tile([P, HALF], F32, name=f"dh_sb{t}_{h}")[:] for t in range(LAST) for h in range(2) if (t, h) != (2, 0)}
+        dh_sb[(2, 0)] = ndz[1][:, 1, :]
+        for t in range(LAST):
+            for h in range(2):
+                nc.scalar.copy(dh_sb[(t, h)], dh[t][:, halves[h]])
+
+        def picked_difference(t, j0, j1):
+            h = j0 // HALF
+            cols = slice(j0 - h * HALF, j1 - h * HALF)
+            nc.vector.tensor_tensor(ndz[h][:, t, cols], tb_pl[t][:].indirect(idx2[:, j0 // 16 : j1 // 16]), dh_sb[(t, h)][:, cols], SUB)
+
+        def plain_difference(h):
+            nc.vector.tensor_tensor(ndz[h][:, LAST, :], tb_last[:, halves[h]], dh[LAST][:, halves[h]], SUB)
+
+        def quantise(j0, j1):
+            h = j0 // HALF
+            nc.vector.quantize_mx(
+                dq_c[:, HALF + j0 : HALF + j1].bitcast(E5M2),
+                dq_s[:, HALF + j0 : HALF + j1],
+                dz_wov[h][:, j0 - h * HALF : j1 - h * HALF, :].rearrange("p j t -> p (j t)"),
+            )
+
+        def second_product(bank, c, first):
+            rows = slice(P * c, P * (c + 1))
+            nc.tensor.matmul_mx(
+                bank[:],
+                lhsT=wu_c[:, rows].bitcast(E4M3),
+                lhsT_scale=wu_s[:, rows],
+                rhs=dq_c[:, first : first + J].bitcast(E5M2),
+                rhs_scale=dq_s[:, first : first + J],
                 start=True,
                 stop=True,
             )
 
-        halves = [slice(0, HALF), slice(HALF, J)]
-        lists = [idx2[:, 0 : HALF // 16], idx2[:, HALF // 16 : J // 16]]
-        tb0 = keep.tile([P, J], F32, name="tb0_pick", tag="shared", align_bytes=64)
-        nc.vector.tensor_copy(tb0[:], tb_pl[0][:].indirect(idx2[:]))
-        dh_sb = [keep.tile([P, J], F32, name=f"dh_sb{t}") for t in range(1, PACK)]
-        for t in range(1, PACK):
-            for h in range(2):
-                nc.scalar.copy(dh_sb[t - 1][:, halves[h]], dh[t][:, halves[h]])
+        def store(copy, bank_cols, c, h):
+            staged = keep.tile([P, HALF], F32, name=f"staged{c}_{h}")
+            copy(staged[:], bank_cols)
+            nc.sync.dma_start(out[P * c : P * (c + 1), halves[h]], staged[:])
 
-        ndz = [keep.tile([P, PACK, HALF], F32, name=f"ndz{h}", align_bytes=64) for h in range(2)]
-        dz_wov = [keep.tile([P, HALF, PACK], BF16, name=f"dz_wov{h}", align_bytes=64) for h in range(2)]
-        dq_c = keep.tile([P, J], U32, name="dq_c", align_bytes=64)
-        dq_s = keep.tile([P, J], U8, name="dq_s", align_bytes=64)
+        picked_difference(0, 0, HALF)
+        for h in range(2):
+            plain_difference(h)
+        for t in range(1, LAST):
+            picked_difference(t, 0, HALF)
+        nc.scalar.activation(*woven(dz_wov[0][:], ndz[0]), COPY, scale=-1.0)
+        free, held = (HALF + QUARTER, J), (HALF, HALF + QUARTER)
 
-        def differences(h):
-            for t in range(1, PACK):
-                nc.vector.tensor_tensor(ndz[h][:, t, :], tb_pl[t][:].indirect(lists[h]), dh_sb[t - 1][:, halves[h]], SUB)
-            nc.vector.tensor_tensor(ndz[h][:, 0, :], tb0[:, halves[h]], dh[0][:, halves[h]], SUB)
+        def quarter_views(j0, j1):
+            return woven(dz_wov[1][:, j0 - HALF : j1 - HALF, :], ndz[1][:, :, j0 - HALF : j1 - HALF])
 
-        def quantise(h):
-            nc.vector.quantize_mx(dq_c[:, halves[h]].bitcast(E5M2), dq_s[:, halves[h]], dz_wov[h][:].rearrange("p j t -> p (j t)"))
+        picked_difference(2, HALF, J)
+        picked_difference(0, *free)
+        picked_difference(1, HALF, J)
+        nc.scalar.activation(*quarter_views(*free), COPY, scale=-1.0)
+        quantise(0, HALF)
+        picked_difference(0, *held)
+        nc.vector.tensor_scalar(*quarter_views(*held), -1.0, None, MULT)
+        quantise(*free)
+        quantise(*held)
 
-        differences(0)
-        d, s = woven(dz_wov[0], ndz[0], 0, HALF)
-        nc.scalar.activation(d, s, COPY, scale=-1.0)
-        differences(1)
-        split = 176
-        d, s = woven(dz_wov[1], ndz[1], 0, split)
-        nc.vector.tensor_scalar(d, s, -1.0, None, MULT)
-        d, s = woven(dz_wov[1], ndz[1], split, HALF)
-        nc.scalar.activation(d, s, COPY, scale=-1.0)
-        quantise(0)
-        quantise(1)
+        for c in range(2):
+            second_product(dh[c], c, 0)
+            store(nc.scalar.copy, dh[c][:, halves[1]], c, 0)
 
         y = [psum.tile([P, J], F32, name=f"y{c}") for c in range(K // P)]
-        y_sb = [keep.tile([P, J], F32, name=f"y_sb{c}") for c in range(K // P)]
-        for c in range(K // P):
-            cols = slice(P * c, P * (c + 1))
-            nc.tensor.matmul_mx(
-                y[c][:],
-                lhsT=wu_c[:, cols].bitcast(E4M3),
-                lhsT_scale=wu_s[:, cols],
-                rhs=dq_c[:].bitcast(E5M2),
-                rhs_scale=dq_s[:],
-                start=True,
-                stop=True,
-            )
-            if c % 2 == 0:
-                nc.scalar.copy(y_sb[c][:], y[c][:])
-            else:
-                nc.vector.tensor_copy(y_sb[c][:], y[c][:])
-            nc.sync.dma_start(out[cols, :], y_sb[c][:])
+        for c in (2, 3, 0, 1):
+            second_product(y[c], c, HALF)
+            copy = nc.scalar.copy if c % 2 == 0 else nc.vector.tensor_copy
+            for h in range(2) if c >= 2 else (1,):
+                store(copy, y[c][:, halves[h]], c, h)

from contextlib import ExitStack

import concourse.mybir as mybir

K, R, N, T, J, V = 512, 512, 512, 1024, 512, 1024
FLOPS = 2 * N * R * J + 2 * R * K * J

F32 = mybir.dt.float32
BF16 = mybir.dt.bfloat16
I32 = mybir.dt.int32
U32 = mybir.dt.uint32
U16 = mybir.dt.uint16
U8 = mybir.dt.uint8
E5M2 = mybir.dt.float8_e5m2_x4
E4M3 = mybir.dt.float8_e4m3fn_x4
E2M1 = mybir.dt.float4_e2m1fn_x4
COPY = mybir.ActivationFunctionType.Copy
SUB = mybir.AluOpType.subtract
MULT = mybir.AluOpType.mult

P = 128
PACK = 4
RUN = 4
HALF = J // 2
QUARTER = J // 4
LAST = PACK - 1


def woven(dst, src):
    d = dst.rearrange("p (c i) t -> p c t i", i=RUN)
    s = src.rearrange("p t (c i) -> p c t i", i=RUN)
    return d, s


def tile_list_gradient_less_table_kernel(tc, g, wd_words, wd_scales, tb, wu_words, wu_scales, offs, offs2, out):
    nc = tc.nc
    with ExitStack() as ctx:
        keep = ctx.enter_context(tc.tile_pool(name="keep", bufs=1))
        psum = ctx.enter_context(tc.psum_pool(name="psum", bufs=1))

        idx = keep.tile([P, J // 16], U16, name="idx")
        idx2 = keep.tile([P, J // 16], U16, name="idx2")
        wd_raw = keep.tile([P, 2 * R], U8, name="wd_raw", align_bytes=64)
        wd_sraw = keep.tile([P, R], U8, name="wd_sraw", align_bytes=64)
        wu_c = keep.tile([P, K], U32, name="wu_c", align_bytes=64)
        wu_s = keep.tile([P, K], U8, name="wu_s", align_bytes=64)
        g_pl = [keep.tile([P, T], F32, name=f"g{t}", tag=f"g{t}", align_bytes=64) for t in range(PACK)]
        tb_pl = [keep.tile([P, V], F32, name=f"tb{t}") for t in range(PACK)]
        dq_c = keep.tile([P, HALF + J], U32, name="dq_c", align_bytes=64)
        dq_s = keep.tile([P, HALF + J], U8, name="dq_s", align_bytes=64)

        g_rows = g.rearrange("(p t) c -> t p c", t=PACK)
        tb_rows = tb.rearrange("(p t) c -> t p c", t=PACK)
        halves = [slice(0, HALF), slice(HALF, J)]
        list_halves = [slice(0, HALF // 16), slice(HALF // 16, J // 16)]

        nc.vector.memset(wd_sraw[:].bitcast(I32), 0)
        nc.gpsimd.memset(wu_s[:].bitcast(I32), 0)
        nc.gpsimd.memset(dq_c[:, 0:HALF], 0)
        nc.gpsimd.memset(dq_s[:, 0:HALF].bitcast(I32), 0)
        for q in range(4):
            nc.scalar.dma_start(wd_sraw[32 * q : 32 * q + 4, :].bitcast(I32), wd_scales[0, 4 * q : 4 * q + 4, :].bitcast(I32))
        for t in range(PACK):
            nc.sync.dma_start(g_pl[t][:], g_rows[t])
            if t == 0:
                nc.sync.dma_start(idx[:], offs)
        nc.sync.dma_start(wd_raw[:].bitcast(I32), wd_words[0].bitcast(I32))
        nc.sync.dma_start(idx2[:], offs2)
        for t in (LAST, 0, 1, 2):
            nc.sync.dma_start(tb_pl[t][:], tb_rows[t])
        nc.sync.dma_start(wu_c[:].bitcast(I32), wu_words[0].rearrange("p n t -> p (n t)").bitcast(I32))
        for q in range(4):
            nc.sync.dma_start(wu_s[32 * q : 32 * q + 4, :].bitcast(I32), wu_scales[0, 4 * q : 4 * q + 4, :].bitcast(I32))

        wd_by_t = wd_raw[:].bitcast(U16).rearrange("p (m t) -> p t m", t=PACK)
        wd_s_by_t = wd_sraw[:].rearrange("p (m t) -> p t m", t=PACK)

        g_pick = keep.tile([P, PACK, J], BF16, name="g_pick", tag="g_pick", align_bytes=64)
        g_wov_tile = keep.tile([P, J * PACK], BF16, name="g_wov", tag="g_wov", align_bytes=64)
        g_wov = [g_wov_tile[:, h * HALF * PACK : (h + 1) * HALF * PACK].rearrange("p (j t) -> p j t", t=PACK) for h in range(2)]
        gq_c = keep.tile([P, J], U32, name="gq_c", align_bytes=64)
        gq_s = keep.tile([P, J], U8, name="gq_s", align_bytes=64)
        for t in range(LAST):
            nc.vector.tensor_copy(g_pick[:, t, :], g_pl[t][:].indirect(idx[:]))
        for h in range(2):
            nc.vector.tensor_copy(g_pick[:, LAST, halves[h]], g_pl[LAST][:].indirect(idx[:, list_halves[h]]))
        wd_c0 = keep.tile([P, 2 * P], U8, name="wd_c0", align_bytes=64)
        wd_s0 = keep.tile([P, P], U8, name="wd_s0", tag="g3", align_bytes=64)
        nc.vector.tensor_copy(wd_c0[:].bitcast(U16), wd_by_t[:, 0, :])
        nc.vector.tensor_copy(wd_s0[:], wd_s_by_t[:, 0, :])
        nc.scalar.copy(*woven(g_wov[0], g_pick[:, :, halves[0]]))
        nc.vector.tensor_copy(*woven(g_wov[1], g_pick[:, :, halves[1]]))
        for h in range(2):
            nc.vector.quantize_mx(gq_c[:, halves[h]].bitcast(E5M2), gq_s[:, halves[h]], g_wov_tile[:, h * HALF * PACK : (h + 1) * HALF * PACK])
        wd_rest = keep.tile([P, LAST * 3 * P], U8, name="wd_rest", tag="g_pick", align_bytes=64)
        wd_c = wd_rest[:, : LAST * 2 * P]
        wd_s = wd_rest[:, LAST * 2 * P :]
        nc.vector.tensor_copy(wd_c.bitcast(U16).rearrange("p (t m) -> p t m", t=LAST), wd_by_t[:, 1:, :])
        nc.vector.tensor_copy(wd_s.rearrange("p (t m) -> p t m", t=LAST), wd_s_by_t[:, 1:, :])

        dh = [psum.tile([P, J], F32, name=f"dh{t}") for t in range(PACK)]
        for t in (0, LAST, 1, 2):
            codes = wd_c0[:] if t == 0 else wd_c[:, 2 * P * (t - 1) : 2 * P * t]
            scales = wd_s0[:] if t == 0 else wd_s[:, P * (t - 1) : P * t]
            nc.tensor.matmul_mx(
                dh[t][:], lhsT=codes.bitcast(E2M1), lhsT_scale=scales, rhs=gq_c[:].bitcast(E5M2), rhs_scale=gq_s[:], start=True, stop=True
            )

        tb_last = keep.tile([P, J], F32, name="tb_last", tag="g_wov", align_bytes=64)
        nc.vector.tensor_copy(tb_last[:], tb_pl[LAST][:].indirect(idx2[:]))

        slots = keep.tile([P, 7 * HALF + QUARTER], F32, name="slots", align_bytes=64)
        ndz = [slots[:, first : first + PACK * HALF].rearrange("p (t j) -> p t j", t=PACK) for first in (0, LAST * HALF + QUARTER)]
        dz_wov = [keep.tile([P, HALF, PACK], BF16, name=f"dz_wov{h}", align_bytes=64) for h in range(2)]

        dh_sb = {(t, h): keep.tile([P, HALF], F32, name=f"dh_sb{t}_{h}")[:] for t in range(LAST) for h in range(2) if (t, h) != (2, 0)}
        dh_sb[(2, 0)] = ndz[1][:, 1, :]
        for t in range(LAST):
            for h in range(2):
                nc.scalar.copy(dh_sb[(t, h)], dh[t][:, halves[h]])

        def picked_difference(t, j0, j1):
            h = j0 // HALF
            cols = slice(j0 - h * HALF, j1 - h * HALF)
            nc.vector.tensor_tensor(ndz[h][:, t, cols], tb_pl[t][:].indirect(idx2[:, j0 // 16 : j1 // 16]), dh_sb[(t, h)][:, cols], SUB)

        def plain_difference(h):
            nc.vector.tensor_tensor(ndz[h][:, LAST, :], tb_last[:, halves[h]], dh[LAST][:, halves[h]], SUB)

        def quantise(j0, j1):
            h = j0 // HALF
            nc.vector.quantize_mx(
                dq_c[:, HALF + j0 : HALF + j1].bitcast(E5M2),
                dq_s[:, HALF + j0 : HALF + j1],
                dz_wov[h][:, j0 - h * HALF : j1 - h * HALF, :].rearrange("p j t -> p (j t)"),
            )

        def second_product(bank, c, first):
            rows = slice(P * c, P * (c + 1))
            nc.tensor.matmul_mx(
                bank[:],
                lhsT=wu_c[:, rows].bitcast(E4M3),
                lhsT_scale=wu_s[:, rows],
                rhs=dq_c[:, first : first + J].bitcast(E5M2),
                rhs_scale=dq_s[:, first : first + J],
                start=True,
                stop=True,
            )

        def store(copy, bank_cols, c, h):
            staged = keep.tile([P, HALF], F32, name=f"staged{c}_{h}")
            copy(staged[:], bank_cols)
            nc.sync.dma_start(out[P * c : P * (c + 1), halves[h]], staged[:])

        picked_difference(0, 0, HALF)
        for h in range(2):
            plain_difference(h)
        for t in range(1, LAST):
            picked_difference(t, 0, HALF)
        nc.scalar.activation(*woven(dz_wov[0][:], ndz[0]), COPY, scale=-1.0)
        free, held = (HALF + QUARTER, J), (HALF, HALF + QUARTER)

        def quarter_views(j0, j1):
            return woven(dz_wov[1][:, j0 - HALF : j1 - HALF, :], ndz[1][:, :, j0 - HALF : j1 - HALF])

        picked_difference(2, HALF, J)
        picked_difference(0, *free)
        picked_difference(1, HALF, J)
        nc.scalar.activation(*quarter_views(*free), COPY, scale=-1.0)
        quantise(0, HALF)
        picked_difference(0, *held)
        nc.vector.tensor_scalar(*quarter_views(*held), -1.0, None, MULT)
        quantise(*free)
        quantise(*held)

        for c in range(2):
            second_product(dh[c], c, 0)
            store(nc.scalar.copy, dh[c][:, halves[1]], c, 0)

        y = [psum.tile([P, J], F32, name=f"y{c}") for c in range(K // P)]
        for c in (2, 3, 0, 1):
            second_product(y[c], c, HALF)
            copy = nc.scalar.copy if c % 2 == 0 else nc.vector.tensor_copy
            for h in range(2) if c >= 2 else (1,):
                store(copy, y[c][:, halves[h]], c, h)
